import numpy as np
import ml_dtypes


def mxq(x, axis, fmt="e4m3"):
    dtype, down = {"e4m3": (ml_dtypes.float8_e4m3fn, 7), "e5m2": (ml_dtypes.float8_e5m2, 14)}[fmt]
    v = np.moveaxis(np.asarray(x, np.float32).astype(ml_dtypes.bfloat16).astype(np.float64), axis, -1)
    blocks = v.reshape(v.shape[:-1] + (-1, 32))
    amax = np.abs(blocks).max(-1, keepdims=True)
    byte = np.maximum(np.where(amax > 0, np.frexp(amax)[1] - 1 + 127, 0) - down, 1)
    scale = np.exp2(byte - 127.0)
    codes = (blocks / scale).astype(np.float32).astype(dtype).astype(np.float64)
    return np.moveaxis((codes * scale).reshape(v.shape), -1, axis)


WIDE = False


def mx_kscale(k):
    if not WIDE:
        return np.ones(k)
    levels = np.array([10, -10, 5, -5, 0])
    if k % 512:
        return np.exp2(np.random.permutation(np.resize(levels, k // 32))).repeat(32)
    a = np.empty((k // 512, 16))
    for p in range(k // 512):
        a[p, :8] = np.random.permutation(np.resize(levels, 8))
        for g in range(8):
            far = levels[np.abs(levels - a[p, g]) >= 10]
            a[p, g + 8] = far[np.random.randint(len(far))]
    return np.exp2(a.ravel()).repeat(32)


def f64(x):
    return np.asarray(x).astype(np.float64)


def striped(idx):
    return np.tile(np.asarray(idx).reshape(-1, 16).T, (8, 1)).astype(np.uint16)


def unstriped(offs):
    return offs[:16].T.reshape(-1).astype(np.int64)


E2M1 = np.array([0.0, 0.5, 1.0, 1.5, 2.0, 3.0, 4.0, 6.0, -0.0, -0.5, -1.0, -1.5, -2.0, -3.0, -4.0, -6.0])


def pack_weight(w, fmt):
    k, n = w.shape
    w = f64(np.asarray(w, np.float32).astype(ml_dtypes.bfloat16)).reshape(k // 32, 32, n)
    amax = np.abs(w).max(1)
    if fmt == "e4m3":
        byte = np.frexp(amax)[1] - 1 + 127 - 7
    else:
        mant, ex = np.frexp(amax / 6.0)
        byte = np.where(mant > 0.5, ex, ex - 1) + 127
    byte = np.clip(np.where(amax > 0, byte, 1), 1, 254)
    scaled = (w * np.exp2(127.0 - byte)[:, None, :]).reshape(k, n).astype(np.float32)
    by_word = np.ascontiguousarray(scaled.reshape(k // 512, 128, 4, n).transpose(0, 1, 3, 2))
    if fmt == "e4m3":
        words = by_word.astype(ml_dtypes.float8_e4m3fn).view(np.uint8)
    else:
        c = by_word.astype(ml_dtypes.float4_e2m1fn).view(np.uint8) & 0xF
        words = (c[..., 0::2] | (c[..., 1::2] << 4)).reshape(k // 512, 128, 2 * n)
    return np.ascontiguousarray(words), np.ascontiguousarray(byte.astype(np.uint8).reshape(k // 512, 16, n))


def unpack_weight(words, scales, fmt):
    g, _, n = scales.shape
    words = np.ascontiguousarray(words).reshape(g, 128, n, -1)
    if fmt == "e4m3":
        vals = words.view(ml_dtypes.float8_e4m3fn).astype(np.float64)
    else:
        nib = np.empty((g, 128, n, 4), np.uint8)
        nib[..., 0::2] = words & 0xF
        nib[..., 1::2] = words >> 4
        vals = E2M1[nib]
    vals = vals * np.repeat(np.exp2(scales.astype(np.float64) - 127.0), 8, axis=1)[..., None]
    return vals.transpose(0, 1, 3, 2).reshape(g * 512, n)


B, N, T, D, NQ = 1, 1024, 4096, 512, 256
SEG = 16


def setup_inputs():
    n = np.random.standard_normal
    jdx = np.random.permutation(1024)[:B * NQ]
    pages = np.random.permutation(T // 16)[:B * N // 16]
    idx = (pages[:, None] * 16 + np.arange(16)[None, :]).reshape(-1)
    s = mx_kscale(D)[:, None]
    kp = pack_weight(n((D, T)) / s, "e4m3")
    return {
        "qT": (n((D, 1024)) * s * (1.00 / np.sqrt(D))).astype(np.float32),
        "k_words": kp[0],
        "k_scales": kp[1],
        "offq": striped(jdx),
        "offs": striped(idx),
    }


def reference(qT, k_words, k_scales, offq, offs):
    jdx = unstriped(offq)
    idx = unstriped(offs)
    pick = lambda x, which: x[:, which].reshape(x.shape[0], B, -1).transpose(1, 0, 2)
    qg = mxq(pick(f64(qT), jdx), 1, "e4m3")
    k = unpack_weight(k_words, k_scales, "e4m3")
    kg = pick(k, idx)
    qq = qg
    a = qq.transpose(0, 2, 1) @ kg
    y = a.reshape(B, NQ, N // SEG, SEG).max(-1)
    return y

@@ -1,0 +1,96 @@
+from contextlib import ExitStack
+
+import concourse.mybir as mybir
+
+F32 = mybir.dt.float32
+BF16 = mybir.dt.bfloat16
+I32 = mybir.dt.int32
+U32 = mybir.dt.uint32
+U16 = mybir.dt.uint16
+U8 = mybir.dt.uint8
+FP8X4 = mybir.dt.float8_e4m3fn_x4
+
+P = 128
+PACK = 4
+POOL_Q = 1024
+POOL_K = 4096
+NQ = 256
+N = 1024
+SEG = 16
+HALF = N // 2
+
+FLOPS = 2 * NQ * N * P * PACK
+
+
+def tile_attend_lq_maxsim_kernel(tc, qT, k_words, k_scales, offq, offs, out):
+    nc = tc.nc
+    with ExitStack() as ctx:
+        keep = ctx.enter_context(tc.tile_pool(name="keep", bufs=1))
+        psum = ctx.enter_context(tc.psum_pool(name="psum", bufs=1))
+
+        q_list = keep.tile([P, NQ // 16], U16, name="q_list")
+        k_list = keep.tile([P, N // 16], U16, name="k_list")
+        q_rows = qT.rearrange("(p t) n -> p t n", t=PACK)
+        q_pool = [keep.tile([P, 2, POOL_Q], F32, name="q_pool%d" % u) for u in range(2)]
+        word_pool = keep.tile([P, POOL_K], U32, name="word_pool", align_bytes=64)
+        scale_pool = keep.tile([P, POOL_K], U8, name="scale_pool", align_bytes=64)
+
+        nc.vector.memset(scale_pool[:].bitcast(I32), 0)
+        nc.sync.dma_start(q_pool[0][:], q_rows[:, 0:2, :])
+        nc.sync.dma_start(k_list[:], offs)
+        nc.sync.dma_start(q_list[:], offq)
+        for quad in range(4):
+            nc.scalar.dma_start(
+                scale_pool[32 * quad : 32 * quad + 4, :].bitcast(I32),
+                k_scales[0, 4 * quad : 4 * quad + 4, :].bitcast(I32),
+            )
+        nc.sync.dma_start(q_pool[1][:], q_rows[:, 2:4, :])
+        nc.sync.dma_start(
+            word_pool[:].bitcast(I32), k_words[0].rearrange("p n r -> p (n r)").bitcast(I32)
+        )
+
+        q_planes = keep.tile([P, PACK, NQ], F32, name="q_planes")
+        k_scale = keep.tile([P, N], U8, name="k_scale", align_bytes=64)
+        for t in range(2):
+            nc.vector.tensor_copy(q_planes[:, t, :], q_pool[0][:, t, :].indirect(q_list[:]))
+        nc.vector.tensor_copy(k_scale[:], scale_pool[:].indirect(k_list[:]))
+        for t in range(2):
+            nc.vector.tensor_copy(q_planes[:, 2 + t, :], q_pool[1][:, t, :].indirect(q_list[:]))
+
+        q_grouped = keep.tile([P, NQ, PACK], BF16, name="q_grouped", align_bytes=64)
+        nc.vector.tensor_copy(q_grouped[:], q_planes[:].rearrange("p t n -> p n t"))
+        q_code = keep.tile([P, NQ], U32, name="q_code", align_bytes=64)
+        q_scale = keep.tile([P, NQ], U8, name="q_scale", align_bytes=64)
+        nc.vector.quantize_mx(
+            out=q_code[:].bitcast(FP8X4),
+            scales=q_scale[:],
+            in_=q_grouped[:].rearrange("p n t -> p (n t)"),
+        )
+
+        k_code = [keep.tile([P, HALF], U32, name="k_code%d" % h, align_bytes=64) for h in range(2)]
+        for h in range(2):
+            cols = slice(h * HALF // 16, (h + 1) * HALF // 16)
+            nc.vector.tensor_copy(k_code[h][:], word_pool[:].indirect(k_list[:, cols]))
+
+        best = [keep.tile([P, N // SEG], F32, name="best%d" % m) for m in range(2)]
+        pieces = [(0, 0, 256), (0, 256, 256), (1, 0, 512), (0, 512, 512), (1, 512, 512)]
+        for i, (m, n0, width) in enumerate(pieces):
+            acc = psum.tile([P, width], F32, name="acc%d" % i)
+            h, c0 = divmod(n0, HALF)
+            nc.tensor.matmul_mx(
+                out=acc[:],
+                lhsT=q_code[:, m * P : (m + 1) * P].bitcast(FP8X4),
+                lhsT_scale=q_scale[:, m * P : (m + 1) * P],
+                rhs=k_code[h][:, c0 : c0 + width].bitcast(FP8X4),
+                rhs_scale=k_scale[:, n0 : n0 + width],
+                start=True,
+                stop=True,
+            )
+            nc.vector.tensor_reduce(
+                out=best[m][:, n0 // SEG : (n0 + width) // SEG],
+                in_=acc[:].rearrange("p (j s) -> p j s", s=SEG),
+                axis=mybir.AxisListType.X,
+                op=mybir.AluOpType.max,
+            )
+            if n0 + width == N:
+                nc.sync.dma_start(out[0, m * P : (m + 1) * P, :], best[m][:])

@@ -31,57 +31,59 @@ def tile_attend_lq_maxsim_kernel(tc, qT, k_words, k_scales, offq, offs, out):
         q_list = keep.tile([P, NQ // 16], U16, name="q_list")
         k_list = keep.tile([P, N // 16], U16, name="k_list")
         q_rows = qT.rearrange("(p t) n -> p t n", t=PACK)
-        q_pool = [keep.tile([P, 2, POOL_Q], F32, name="q_pool%d" % u) for u in range(2)]
+        q_pool = keep.tile([P, PACK, POOL_Q], F32, name="q_pool")
         word_pool = keep.tile([P, POOL_K], U32, name="word_pool", align_bytes=64)
         scale_pool = keep.tile([P, POOL_K], U8, name="scale_pool", align_bytes=64)
 
         nc.vector.memset(scale_pool[:].bitcast(I32), 0)
-        nc.sync.dma_start(q_pool[0][:], q_rows[:, 0:2, :])
         nc.sync.dma_start(k_list[:], offs)
         nc.sync.dma_start(q_list[:], offq)
-        for quad in range(4):
-            nc.scalar.dma_start(
-                scale_pool[32 * quad : 32 * quad + 4, :].bitcast(I32),
-                k_scales[0, 4 * quad : 4 * quad + 4, :].bitcast(I32),
-            )
-        nc.sync.dma_start(q_pool[1][:], q_rows[:, 2:4, :])
+        nc.scalar.dma_start(scale_pool[4:P:8, :].bitcast(I32), k_scales[0].bitcast(I32))
         nc.sync.dma_start(
             word_pool[:].bitcast(I32), k_words[0].rearrange("p n r -> p (n r)").bitcast(I32)
         )
+        nc.sync.dma_start(q_pool[:, 0:2, :], q_rows[:, 0:2, :])
+        nc.sync.dma_start(q_pool[:, 2, :], q_rows[:, 2, :])
+        nc.sync.dma_start(q_pool[:, 3, :], q_rows[:, 3, :])
 
-        q_planes = keep.tile([P, PACK, NQ], F32, name="q_planes")
         k_scale = keep.tile([P, N], U8, name="k_scale", align_bytes=64)
-        for t in range(2):
-            nc.vector.tensor_copy(q_planes[:, t, :], q_pool[0][:, t, :].indirect(q_list[:]))
-        nc.vector.tensor_copy(k_scale[:], scale_pool[:].indirect(k_list[:]))
-        for t in range(2):
-            nc.vector.tensor_copy(q_planes[:, 2 + t, :], q_pool[1][:, t, :].indirect(q_list[:]))
+        picked_scale = keep.tile([P, N], U8, name="picked_scale", align_bytes=64)
+        nc.vector.tensor_copy(picked_scale[:], scale_pool[:].indirect(k_list[:]))
+        for quad in range(4):
+            nc.scalar.dma_start(
+                k_scale[32 * quad : 32 * quad + 4, :].bitcast(I32),
+                picked_scale[32 * quad + 4 : 32 * quad + 32 : 8, :].bitcast(I32),
+            )
+        k_code = [keep.tile([P, N], U32, name="k_code", align_bytes=64)]
+        nc.vector.tensor_copy(k_code[0][:], word_pool[:].indirect(k_list[:]))
 
-        q_grouped = keep.tile([P, NQ, PACK], BF16, name="q_grouped", align_bytes=64)
-        nc.vector.tensor_copy(q_grouped[:], q_planes[:].rearrange("p t n -> p n t"))
+        q_pair = keep.tile([P, 2, NQ], F32, name="q_pair")
+        for t in range(2):
+            nc.vector.tensor_copy(q_pair[:, t, :], q_pool[:, t, :].indirect(q_list[:]))
+        q_grouped = [keep.tile([P, P, PACK], BF16, name="q_grouped%d" % m, align_bytes=64) for m in range(2)]
         q_code = keep.tile([P, NQ], U32, name="q_code", align_bytes=64)
         q_scale = keep.tile([P, NQ], U8, name="q_scale", align_bytes=64)
-        nc.vector.quantize_mx(
-            out=q_code[:].bitcast(FP8X4),
-            scales=q_scale[:],
-            in_=q_grouped[:].rearrange("p n t -> p (n t)"),
-        )
-
-        k_code = [keep.tile([P, HALF], U32, name="k_code%d" % h, align_bytes=64) for h in range(2)]
-        for h in range(2):
-            cols = slice(h * HALF // 16, (h + 1) * HALF // 16)
-            nc.vector.tensor_copy(k_code[h][:], word_pool[:].indirect(k_list[:, cols]))
+        for m in range(2):
+            nc.scalar.copy(q_grouped[m][:, :, 0:2], q_pair[:, :, m * P : (m + 1) * P].rearrange("p t n -> p n t"))
+        for m in range(2):
+            nc.vector.tensor_copy(q_grouped[m][:, :, 2], q_pool[:, 2, :].indirect(q_list[:, m * 8 : (m + 1) * 8]))
+        for m in range(2):
+            nc.vector.tensor_copy(q_grouped[m][:, :, 3], q_pool[:, 3, :].indirect(q_list[:, m * 8 : (m + 1) * 8]))
+            nc.vector.quantize_mx(
+                out=q_code[:, m * P : (m + 1) * P].bitcast(FP8X4),
+                scales=q_scale[:, m * P : (m + 1) * P],
+                in_=q_grouped[m][:].rearrange("p n t -> p (n t)"),
+            )
 
         best = [keep.tile([P, N // SEG], F32, name="best%d" % m) for m in range(2)]
-        pieces = [(0, 0, 256), (0, 256, 256), (1, 0, 512), (0, 512, 512), (1, 512, 512)]
+        pieces = [(m, n0, 256) for m in range(2) for n0 in range(0, N, 256)]
         for i, (m, n0, width) in enumerate(pieces):
             acc = psum.tile([P, width], F32, name="acc%d" % i)
-            h, c0 = divmod(n0, HALF)
             nc.tensor.matmul_mx(
                 out=acc[:],
                 lhsT=q_code[:, m * P : (m + 1) * P].bitcast(FP8X4),
                 lhsT_scale=q_scale[:, m * P : (m + 1) * P],
-                rhs=k_code[h][:, c0 : c0 + width].bitcast(FP8X4),
+                rhs=k_code[0][:, n0 : n0 + width].bitcast(FP8X4),
                 rhs_scale=k_scale[:, n0 : n0 + width],
                 start=True,
                 stop=True,

@@ -36,21 +36,21 @@ def tile_attend_lq_maxsim_kernel(tc, qT, k_words, k_scales, offq, offs, out):
         scale_pool = keep.tile([P, POOL_K], U8, name="scale_pool", align_bytes=64)
 
         nc.vector.memset(scale_pool[:].bitcast(I32), 0)
-        nc.sync.dma_start(k_list[:], offs)
-        nc.sync.dma_start(q_list[:], offq)
-        nc.scalar.dma_start(scale_pool[4:P:8, :].bitcast(I32), k_scales[0].bitcast(I32))
-        nc.sync.dma_start(
+        nc.scalar.dma_start(
             word_pool[:].bitcast(I32), k_words[0].rearrange("p n r -> p (n r)").bitcast(I32)
         )
-        nc.sync.dma_start(q_pool[:, 0:2, :], q_rows[:, 0:2, :])
-        nc.sync.dma_start(q_pool[:, 2, :], q_rows[:, 2, :])
-        nc.sync.dma_start(q_pool[:, 3, :], q_rows[:, 3, :])
+        nc.sync.dma_start(k_list[:], offs)
+        nc.sync.dma_start(q_list[:], offq)
+        nc.sync.dma_start(scale_pool[4:P:8, :].bitcast(I32), k_scales[0].bitcast(I32))
+        nc.scalar.dma_start(q_pool[:, 0:2, :], q_rows[:, 0:2, :])
+        nc.scalar.dma_start(q_pool[:, 2, :], q_rows[:, 2, :])
+        nc.scalar.dma_start(q_pool[:, 3, :], q_rows[:, 3, :])
 
         k_scale = keep.tile([P, N], U8, name="k_scale", align_bytes=64)
         picked_scale = keep.tile([P, N], U8, name="picked_scale", align_bytes=64)
         nc.vector.tensor_copy(picked_scale[:], scale_pool[:].indirect(k_list[:]))
         for quad in range(4):
-            nc.scalar.dma_start(
+            nc.sync.dma_start(
                 k_scale[32 * quad : 32 * quad + 4, :].bitcast(I32),
                 picked_scale[32 * quad + 4 : 32 * quad + 32 : 8, :].bitcast(I32),
             )

@@ -9,6 +9,7 @@ U32 = mybir.dt.uint32
 U16 = mybir.dt.uint16
 U8 = mybir.dt.uint8
 FP8X4 = mybir.dt.float8_e4m3fn_x4
+COPY = mybir.ActivationFunctionType.Copy
 
 P = 128
 PACK = 4
@@ -57,14 +58,16 @@ def tile_attend_lq_maxsim_kernel(tc, qT, k_words, k_scales, offq, offs, out):
         k_code = [keep.tile([P, N], U32, name="k_code", align_bytes=64)]
         nc.vector.tensor_copy(k_code[0][:], word_pool[:].indirect(k_list[:]))
 
-        q_pair = keep.tile([P, 2, NQ], F32, name="q_pair")
-        for t in range(2):
-            nc.vector.tensor_copy(q_pair[:, t, :], q_pool[:, t, :].indirect(q_list[:]))
+        q_one = keep.tile([P, NQ], F32, name="q_one")
+        nc.vector.tensor_copy(q_one[:], q_pool[:, 1, :].indirect(q_list[:]))
+        q_zero = keep.tile([P, POOL_Q], BF16, name="q_zero", align_bytes=64)
+        nc.scalar.activation(q_zero[:], q_pool[:, 0, :], COPY)
         q_grouped = [keep.tile([P, P, PACK], BF16, name="q_grouped%d" % m, align_bytes=64) for m in range(2)]
         q_code = keep.tile([P, NQ], U32, name="q_code", align_bytes=64)
         q_scale = keep.tile([P, NQ], U8, name="q_scale", align_bytes=64)
         for m in range(2):
-            nc.scalar.copy(q_grouped[m][:, :, 0:2], q_pair[:, :, m * P : (m + 1) * P].rearrange("p t n -> p n t"))
+            nc.scalar.activation(q_grouped[m][:, :, 0], q_zero[:].indirect(q_list[:, m * 8 : (m + 1) * 8]), COPY)
+            nc.scalar.copy(q_grouped[m][:, :, 1], q_one[:, m * P : (m + 1) * P])
         for m in range(2):
             nc.vector.tensor_copy(q_grouped[m][:, :, 2], q_pool[:, 2, :].indirect(q_list[:, m * 8 : (m + 1) * 8]))
         for m in range(2):

@@ -18,7 +18,7 @@ POOL_K = 4096
 NQ = 256
 N = 1024
 SEG = 16
-HALF = N // 2
+LEAD = 3 * POOL_K // 8
 
 FLOPS = 2 * NQ * N * P * PACK
 
@@ -37,12 +37,12 @@ def tile_attend_lq_maxsim_kernel(tc, qT, k_words, k_scales, offq, offs, out):
         scale_pool = keep.tile([P, POOL_K], U8, name="scale_pool", align_bytes=64)
 
         nc.vector.memset(scale_pool[:].bitcast(I32), 0)
-        nc.scalar.dma_start(
-            word_pool[:].bitcast(I32), k_words[0].rearrange("p n r -> p (n r)").bitcast(I32)
-        )
+        words = k_words[0].rearrange("p n r -> p (n r)").bitcast(I32)
+        nc.scalar.dma_start(word_pool[:, :LEAD].bitcast(I32), words[:, :LEAD])
         nc.sync.dma_start(k_list[:], offs)
         nc.sync.dma_start(q_list[:], offq)
-        nc.sync.dma_start(scale_pool[4:P:8, :].bitcast(I32), k_scales[0].bitcast(I32))
+        nc.scalar.dma_start(scale_pool[4:P:8, :].bitcast(I32), k_scales[0].bitcast(I32))
+        nc.scalar.dma_start(word_pool[:, LEAD:].bitcast(I32), words[:, LEAD:])
         nc.scalar.dma_start(q_pool[:, 0:2, :], q_rows[:, 0:2, :])
         nc.scalar.dma_start(q_pool[:, 2, :], q_rows[:, 2, :])
         nc.scalar.dma_start(q_pool[:, 3, :], q_rows[:, 3, :])

@@ -51,7 +51,8 @@ def tile_attend_lq_maxsim_kernel(tc, qT, k_words, k_scales, offq, offs, out):
         picked_scale = keep.tile([P, N], U8, name="picked_scale", align_bytes=64)
         nc.vector.tensor_copy(picked_scale[:], scale_pool[:].indirect(k_list[:]))
         for quad in range(4):
-            nc.sync.dma_start(
+            queue = nc.sync if quad < 2 else nc.scalar
+            queue.dma_start(
                 k_scale[32 * quad : 32 * quad + 4, :].bitcast(I32),
                 picked_scale[32 * quad + 4 : 32 * quad + 32 : 8, :].bitcast(I32),
             )

@@ -50,11 +50,12 @@ def tile_attend_lq_maxsim_kernel(tc, qT, k_words, k_scales, offq, offs, out):
         k_scale = keep.tile([P, N], U8, name="k_scale", align_bytes=64)
         picked_scale = keep.tile([P, N], U8, name="picked_scale", align_bytes=64)
         nc.vector.tensor_copy(picked_scale[:], scale_pool[:].indirect(k_list[:]))
-        for quad in range(4):
-            queue = nc.sync if quad < 2 else nc.scalar
+        nc.vector.tensor_copy(k_scale[:].bitcast(I32), picked_scale[:].bitcast(I32))
+        for r in range(1, 4):
+            queue = nc.sync if r == 1 else nc.scalar
             queue.dma_start(
-                k_scale[32 * quad : 32 * quad + 4, :].bitcast(I32),
-                picked_scale[32 * quad + 4 : 32 * quad + 32 : 8, :].bitcast(I32),
+                k_scale[4 + r : P : 32, :].bitcast(I32),
+                picked_scale[4 + 8 * r : P : 32, :].bitcast(I32),
             )
         k_code = [keep.tile([P, N], U32, name="k_code", align_bytes=64)]
         nc.vector.tensor_copy(k_code[0][:], word_pool[:].indirect(k_list[:]))
@@ -88,7 +89,7 @@ def tile_attend_lq_maxsim_kernel(tc, qT, k_words, k_scales, offq, offs, out):
                 lhsT=q_code[:, m * P : (m + 1) * P].bitcast(FP8X4),
                 lhsT_scale=q_scale[:, m * P : (m + 1) * P],
                 rhs=k_code[0][:, n0 : n0 + width].bitcast(FP8X4),
-                rhs_scale=k_scale[:, n0 : n0 + width],
+                rhs_scale=k_scale[4:P, n0 : n0 + width],
                 start=True,
                 stop=True,
             )

@@ -60,6 +60,18 @@ def tile_attend_lq_maxsim_kernel(tc, qT, k_words, k_scales, offq, offs, out):
         k_code = [keep.tile([P, N], U32, name="k_code", align_bytes=64)]
         nc.vector.tensor_copy(k_code[0][:], word_pool[:].indirect(k_list[:]))
 
+        warm = psum.tile([P, 512], F32, name="warm", tag="acc7")
+        for w in range(4):
+            nc.tensor.matmul_mx(
+                out=warm[0:32, :],
+                lhsT=k_code[0][:, 0:32].bitcast(FP8X4),
+                lhsT_scale=picked_scale[:, 0:32],
+                rhs=k_code[0][:, 0:512].bitcast(FP8X4),
+                rhs_scale=picked_scale[:, 0:512],
+                start=True,
+                stop=True,
+            )
+
         q_one = keep.tile([P, NQ], F32, name="q_one")
         nc.vector.tensor_copy(q_one[:], q_pool[:, 1, :].indirect(q_list[:]))
         q_zero = keep.tile([P, POOL_Q], BF16, name="q_zero", align_bytes=64)
@@ -83,7 +95,7 @@ def tile_attend_lq_maxsim_kernel(tc, qT, k_words, k_scales, offq, offs, out):
         best = [keep.tile([P, N // SEG], F32, name="best%d" % m) for m in range(2)]
         pieces = [(m, n0, 256) for m in range(2) for n0 in range(0, N, 256)]
         for i, (m, n0, width) in enumerate(pieces):
-            acc = psum.tile([P, width], F32, name="acc%d" % i)
+            acc = psum.tile([P, width], F32, name="acc%d" % i, tag="acc%d" % i)
             nc.tensor.matmul_mx(
                 out=acc[:],
                 lhsT=q_code[:, m * P : (m + 1) * P].bitcast(FP8X4),

@@ -41,7 +41,7 @@ def tile_attend_lq_maxsim_kernel(tc, qT, k_words, k_scales, offq, offs, out):
         nc.scalar.dma_start(word_pool[:, :LEAD].bitcast(I32), words[:, :LEAD])
         nc.sync.dma_start(k_list[:], offs)
         nc.sync.dma_start(q_list[:], offq)
-        nc.scalar.dma_start(scale_pool[4:P:8, :].bitcast(I32), k_scales[0].bitcast(I32))
+        nc.scalar.dma_start(scale_pool[11 : 11 + 7 * 15 + 1 : 7, :].bitcast(I32), k_scales[0].bitcast(I32))
         nc.scalar.dma_start(word_pool[:, LEAD:].bitcast(I32), words[:, LEAD:])
         nc.scalar.dma_start(q_pool[:, 0:2, :], q_rows[:, 0:2, :])
         nc.scalar.dma_start(q_pool[:, 2, :], q_rows[:, 2, :])
@@ -50,12 +50,11 @@ def tile_attend_lq_maxsim_kernel(tc, qT, k_words, k_scales, offq, offs, out):
         k_scale = keep.tile([P, N], U8, name="k_scale", align_bytes=64)
         picked_scale = keep.tile([P, N], U8, name="picked_scale", align_bytes=64)
         nc.vector.tensor_copy(picked_scale[:], scale_pool[:].indirect(k_list[:]))
-        nc.vector.tensor_copy(k_scale[:].bitcast(I32), picked_scale[:].bitcast(I32))
-        for r in range(1, 4):
-            queue = nc.sync if r == 1 else nc.scalar
+        for r in range(4):
+            queue = nc.sync if r < 2 else nc.scalar
             queue.dma_start(
-                k_scale[4 + r : P : 32, :].bitcast(I32),
-                picked_scale[4 + 8 * r : P : 32, :].bitcast(I32),
+                k_scale[r:P:32, :].bitcast(I32),
+                picked_scale[11 + 7 * r : 11 + 7 * r + 28 * 3 + 1 : 28, :].bitcast(I32),
             )
         k_code = [keep.tile([P, N], U32, name="k_code", align_bytes=64)]
         nc.vector.tensor_copy(k_code[0][:], word_pool[:].indirect(k_list[:]))
@@ -93,7 +92,7 @@ def tile_attend_lq_maxsim_kernel(tc, qT, k_words, k_scales, offq, offs, out):
             )
 
         best = [keep.tile([P, N // SEG], F32, name="best%d" % m) for m in range(2)]
-        pieces = [(m, n0, 256) for m in range(2) for n0 in range(0, N, 256)]
+        pieces = [(0, 0, 128), (0, 128, 128), (0, 256, 256), (0, 512, 512), (1, 0, 512), (1, 512, 512)]
         for i, (m, n0, width) in enumerate(pieces):
             acc = psum.tile([P, width], F32, name="acc%d" % i, tag="acc%d" % i)
             nc.tensor.matmul_mx(
@@ -101,7 +100,7 @@ def tile_attend_lq_maxsim_kernel(tc, qT, k_words, k_scales, offq, offs, out):
                 lhsT=q_code[:, m * P : (m + 1) * P].bitcast(FP8X4),
                 lhsT_scale=q_scale[:, m * P : (m + 1) * P],
                 rhs=k_code[0][:, n0 : n0 + width].bitcast(FP8X4),
-                rhs_scale=k_scale[4:P, n0 : n0 + width],
+                rhs_scale=k_scale[:, n0 : n0 + width],
                 start=True,
                 stop=True,
             )

@@ -92,7 +92,7 @@ def tile_attend_lq_maxsim_kernel(tc, qT, k_words, k_scales, offq, offs, out):
             )
 
         best = [keep.tile([P, N // SEG], F32, name="best%d" % m) for m in range(2)]
-        pieces = [(0, 0, 128), (0, 128, 128), (0, 256, 256), (0, 512, 512), (1, 0, 512), (1, 512, 512)]
+        pieces = [(m, n0, 256) for m in range(2) for n0 in range(0, N, 256)]
         for i, (m, n0, width) in enumerate(pieces):
             acc = psum.tile([P, width], F32, name="acc%d" % i, tag="acc%d" % i)
             nc.tensor.matmul_mx(

@@ -18,7 +18,7 @@ POOL_K = 4096
 NQ = 256
 N = 1024
 SEG = 16
-LEAD = 3 * POOL_K // 8
+LEAD = POOL_K // 2
 
 FLOPS = 2 * NQ * N * P * PACK
 
@@ -59,18 +59,6 @@ def tile_attend_lq_maxsim_kernel(tc, qT, k_words, k_scales, offq, offs, out):
         k_code = [keep.tile([P, N], U32, name="k_code", align_bytes=64)]
         nc.vector.tensor_copy(k_code[0][:], word_pool[:].indirect(k_list[:]))
 
-        warm = psum.tile([P, 512], F32, name="warm", tag="acc7")
-        for w in range(4):
-            nc.tensor.matmul_mx(
-                out=warm[0:32, :],
-                lhsT=k_code[0][:, 0:32].bitcast(FP8X4),
-                lhsT_scale=picked_scale[:, 0:32],
-                rhs=k_code[0][:, 0:512].bitcast(FP8X4),
-                rhs_scale=picked_scale[:, 0:512],
-                start=True,
-                stop=True,
-            )
-
         q_one = keep.tile([P, NQ], F32, name="q_one")
         nc.vector.tensor_copy(q_one[:], q_pool[:, 1, :].indirect(q_list[:]))
         q_zero = keep.tile([P, POOL_Q], BF16, name="q_zero", align_bytes=64)
@@ -110,5 +98,9 @@ def tile_attend_lq_maxsim_kernel(tc, qT, k_words, k_scales, offq, offs, out):
                 axis=mybir.AxisListType.X,
                 op=mybir.AluOpType.max,
             )
-            if n0 + width == N:
-                nc.sync.dma_start(out[0, m * P : (m + 1) * P, :], best[m][:])
+            if m == 0 and n0 + width == N:
+                nc.sync.dma_start(out[0, 0:P, :], best[0][:])
+            if m == 1 and n0 + 2 * width == N:
+                nc.scalar.dma_start(out[0, P:NQ, 0:48], best[1][:, 0:48])
+            if m == 1 and n0 + width == N:
+                nc.sync.dma_start(out[0, P:NQ, 48:64], best[1][:, 48:64])

@@ -18,7 +18,7 @@ POOL_K = 4096
 NQ = 256
 N = 1024
 SEG = 16
-LEAD = POOL_K // 2
+LEAD = 3 * POOL_K // 8
 
 FLOPS = 2 * NQ * N * P * PACK
 

@@ -32,7 +32,8 @@ def tile_attend_lq_maxsim_kernel(tc, qT, k_words, k_scales, offq, offs, out):
         q_list = keep.tile([P, NQ // 16], U16, name="q_list")
         k_list = keep.tile([P, N // 16], U16, name="k_list")
         q_rows = qT.rearrange("(p t) n -> p t n", t=PACK)
-        q_pool = keep.tile([P, PACK, POOL_Q], F32, name="q_pool")
+        q_first = keep.tile([P, POOL_Q], F32, name="q_first")
+        q_pool = keep.tile([P, PACK - 1, POOL_Q], F32, name="q_pool")
         word_pool = keep.tile([P, POOL_K], U32, name="word_pool", align_bytes=64)
         scale_pool = keep.tile([P, POOL_K], U8, name="scale_pool", align_bytes=64)
 
@@ -43,9 +44,9 @@ def tile_attend_lq_maxsim_kernel(tc, qT, k_words, k_scales, offq, offs, out):
         nc.sync.dma_start(q_list[:], offq)
         nc.scalar.dma_start(scale_pool[11 : 11 + 7 * 15 + 1 : 7, :].bitcast(I32), k_scales[0].bitcast(I32))
         nc.scalar.dma_start(word_pool[:, LEAD:].bitcast(I32), words[:, LEAD:])
-        nc.scalar.dma_start(q_pool[:, 0:2, :], q_rows[:, 0:2, :])
-        nc.scalar.dma_start(q_pool[:, 2, :], q_rows[:, 2, :])
-        nc.scalar.dma_start(q_pool[:, 3, :], q_rows[:, 3, :])
+        nc.scalar.dma_start(q_pool[:, 0:2, :], q_rows[:, 1:3, :])
+        nc.scalar.dma_start(q_first[:], q_rows[:, 0, :])
+        nc.scalar.dma_start(q_pool[:, 2, :], q_rows[:, 3, :])
 
         k_scale = keep.tile([P, N], U8, name="k_scale", align_bytes=64)
         picked_scale = keep.tile([P, N], U8, name="picked_scale", align_bytes=64)
@@ -59,20 +60,20 @@ def tile_attend_lq_maxsim_kernel(tc, qT, k_words, k_scales, offq, offs, out):
         k_code = [keep.tile([P, N], U32, name="k_code", align_bytes=64)]
         nc.vector.tensor_copy(k_code[0][:], word_pool[:].indirect(k_list[:]))
 
-        q_one = keep.tile([P, NQ], F32, name="q_one")
-        nc.vector.tensor_copy(q_one[:], q_pool[:, 1, :].indirect(q_list[:]))
-        q_zero = keep.tile([P, POOL_Q], BF16, name="q_zero", align_bytes=64)
-        nc.scalar.activation(q_zero[:], q_pool[:, 0, :], COPY)
         q_grouped = [keep.tile([P, P, PACK], BF16, name="q_grouped%d" % m, align_bytes=64) for m in range(2)]
         q_code = keep.tile([P, NQ], U32, name="q_code", align_bytes=64)
         q_scale = keep.tile([P, NQ], U8, name="q_scale", align_bytes=64)
+        q_one = keep.tile([P, POOL_Q], BF16, name="q_one", align_bytes=64)
+        nc.scalar.activation(q_one[:], q_pool[:, 0, :], COPY)
+        picked = [keep.tile([P, 2, P], BF16, name="picked%d" % m) for m in range(2)]
         for m in range(2):
-            nc.scalar.activation(q_grouped[m][:, :, 0], q_zero[:].indirect(q_list[:, m * 8 : (m + 1) * 8]), COPY)
-            nc.scalar.copy(q_grouped[m][:, :, 1], q_one[:, m * P : (m + 1) * P])
+            nc.scalar.activation(picked[m][:, 1, :], q_one[:].indirect(q_list[:, m * 8 : (m + 1) * 8]), COPY)
+            nc.vector.tensor_copy(q_grouped[m][:, :, 2], q_pool[:, 1, :].indirect(q_list[:, m * 8 : (m + 1) * 8]))
         for m in range(2):
-            nc.vector.tensor_copy(q_grouped[m][:, :, 2], q_pool[:, 2, :].indirect(q_list[:, m * 8 : (m + 1) * 8]))
+            nc.vector.tensor_copy(picked[m][:, 0, :], q_first[:].indirect(q_list[:, m * 8 : (m + 1) * 8]))
+            nc.scalar.copy(q_grouped[m][:, :, 0:2], picked[m][:].rearrange("p t n -> p n t"))
         for m in range(2):
-            nc.vector.tensor_copy(q_grouped[m][:, :, 3], q_pool[:, 3, :].indirect(q_list[:, m * 8 : (m + 1) * 8]))
+            nc.vector.tensor_copy(q_grouped[m][:, :, 3], q_pool[:, 2, :].indirect(q_list[:, m * 8 : (m + 1) * 8]))
             nc.vector.quantize_mx(
                 out=q_code[:, m * P : (m + 1) * P].bitcast(FP8X4),
                 scales=q_scale[:, m * P : (m + 1) * P],

@@ -52,8 +52,7 @@ def tile_attend_lq_maxsim_kernel(tc, qT, k_words, k_scales, offq, offs, out):
         picked_scale = keep.tile([P, N], U8, name="picked_scale", align_bytes=64)
         nc.vector.tensor_copy(picked_scale[:], scale_pool[:].indirect(k_list[:]))
         for r in range(4):
-            queue = nc.sync if r < 2 else nc.scalar
-            queue.dma_start(
+            nc.scalar.dma_start(
                 k_scale[r:P:32, :].bitcast(I32),
                 picked_scale[11 + 7 * r : 11 + 7 * r + 28 * 3 + 1 : 28, :].bitcast(I32),
             )

@@ -9,7 +9,6 @@ U32 = mybir.dt.uint32
 U16 = mybir.dt.uint16
 U8 = mybir.dt.uint8
 FP8X4 = mybir.dt.float8_e4m3fn_x4
-COPY = mybir.ActivationFunctionType.Copy
 
 P = 128
 PACK = 4
@@ -18,7 +17,6 @@ POOL_K = 4096
 NQ = 256
 N = 1024
 SEG = 16
-LEAD = 3 * POOL_K // 8
 
 FLOPS = 2 * NQ * N * P * PACK
 
@@ -32,21 +30,24 @@ def tile_attend_lq_maxsim_kernel(tc, qT, k_words, k_scales, offq, offs, out):
         q_list = keep.tile([P, NQ // 16], U16, name="q_list")
         k_list = keep.tile([P, N // 16], U16, name="k_list")
         q_rows = qT.rearrange("(p t) n -> p t n", t=PACK)
-        q_first = keep.tile([P, POOL_Q], F32, name="q_first")
-        q_pool = keep.tile([P, PACK - 1, POOL_Q], F32, name="q_pool")
+        q_first = keep.tile([P, 2, POOL_Q], F32, name="q_first")
+        q_pool = keep.tile([P, 2, POOL_Q], F32, name="q_pool")
         word_pool = keep.tile([P, POOL_K], U32, name="word_pool", align_bytes=64)
         scale_pool = keep.tile([P, POOL_K], U8, name="scale_pool", align_bytes=64)
 
         nc.vector.memset(scale_pool[:].bitcast(I32), 0)
         words = k_words[0].rearrange("p n r -> p (n r)").bitcast(I32)
-        nc.scalar.dma_start(word_pool[:, :LEAD].bitcast(I32), words[:, :LEAD])
+        nc.scalar.dma_start(q_first[:], q_rows[:, 0:2, :])
         nc.sync.dma_start(k_list[:], offs)
         nc.sync.dma_start(q_list[:], offq)
         nc.scalar.dma_start(scale_pool[11 : 11 + 7 * 15 + 1 : 7, :].bitcast(I32), k_scales[0].bitcast(I32))
-        nc.scalar.dma_start(word_pool[:, LEAD:].bitcast(I32), words[:, LEAD:])
-        nc.scalar.dma_start(q_pool[:, 0:2, :], q_rows[:, 1:3, :])
-        nc.scalar.dma_start(q_first[:], q_rows[:, 0, :])
-        nc.scalar.dma_start(q_pool[:, 2, :], q_rows[:, 3, :])
+        nc.scalar.dma_start(q_pool[:], q_rows[:, 2:4, :])
+        nc.scalar.dma_start(word_pool[:].bitcast(I32), words)
+
+        q_grouped = [keep.tile([P, P, PACK], BF16, name="q_grouped%d" % m, align_bytes=64) for m in range(2)]
+        for m in range(2):
+            for t in range(2):
+                nc.vector.tensor_copy(q_grouped[m][:, :, t], q_first[:, t, :].indirect(q_list[:, m * 8 : (m + 1) * 8]))
 
         k_scale = keep.tile([P, N], U8, name="k_scale", align_bytes=64)
         picked_scale = keep.tile([P, N], U8, name="picked_scale", align_bytes=64)
@@ -56,38 +57,33 @@ def tile_attend_lq_maxsim_kernel(tc, qT, k_words, k_scales, offq, offs, out):
                 k_scale[r:P:32, :].bitcast(I32),
                 picked_scale[11 + 7 * r : 11 + 7 * r + 28 * 3 + 1 : 28, :].bitcast(I32),
             )
-        k_code = [keep.tile([P, N], U32, name="k_code", align_bytes=64)]
-        nc.vector.tensor_copy(k_code[0][:], word_pool[:].indirect(k_list[:]))
 
-        q_grouped = [keep.tile([P, P, PACK], BF16, name="q_grouped%d" % m, align_bytes=64) for m in range(2)]
         q_code = keep.tile([P, NQ], U32, name="q_code", align_bytes=64)
         q_scale = keep.tile([P, NQ], U8, name="q_scale", align_bytes=64)
-        q_one = keep.tile([P, POOL_Q], BF16, name="q_one", align_bytes=64)
-        nc.scalar.activation(q_one[:], q_pool[:, 0, :], COPY)
-        picked = [keep.tile([P, 2, P], BF16, name="picked%d" % m) for m in range(2)]
         for m in range(2):
-            nc.scalar.activation(picked[m][:, 1, :], q_one[:].indirect(q_list[:, m * 8 : (m + 1) * 8]), COPY)
-            nc.vector.tensor_copy(q_grouped[m][:, :, 2], q_pool[:, 1, :].indirect(q_list[:, m * 8 : (m + 1) * 8]))
+            for t in range(2, PACK):
+                nc.vector.tensor_copy(q_grouped[m][:, :, t], q_pool[:, t - 2, :].indirect(q_list[:, m * 8 : (m + 1) * 8]))
         for m in range(2):
-            nc.vector.tensor_copy(picked[m][:, 0, :], q_first[:].indirect(q_list[:, m * 8 : (m + 1) * 8]))
-            nc.scalar.copy(q_grouped[m][:, :, 0:2], picked[m][:].rearrange("p t n -> p n t"))
-        for m in range(2):
-            nc.vector.tensor_copy(q_grouped[m][:, :, 3], q_pool[:, 2, :].indirect(q_list[:, m * 8 : (m + 1) * 8]))
             nc.vector.quantize_mx(
                 out=q_code[:, m * P : (m + 1) * P].bitcast(FP8X4),
                 scales=q_scale[:, m * P : (m + 1) * P],
                 in_=q_grouped[m][:].rearrange("p n t -> p (n t)"),
             )
 
+        half = N // 2
+        k_code = [keep.tile([P, half], U32, name="k_code%d" % h, align_bytes=64) for h in range(2)]
+        for h in range(2):
+            nc.vector.tensor_copy(k_code[h][:], word_pool[:].indirect(k_list[:, h * half // 16 : (h + 1) * half // 16]))
+
         best = [keep.tile([P, N // SEG], F32, name="best%d" % m) for m in range(2)]
-        pieces = [(m, n0, 256) for m in range(2) for n0 in range(0, N, 256)]
+        pieces = [(0, 0, 256), (0, 256, 256), (1, 0, 512), (0, 512, 512), (1, 512, 256), (1, 768, 256)]
         for i, (m, n0, width) in enumerate(pieces):
             acc = psum.tile([P, width], F32, name="acc%d" % i, tag="acc%d" % i)
             nc.tensor.matmul_mx(
                 out=acc[:],
                 lhsT=q_code[:, m * P : (m + 1) * P].bitcast(FP8X4),
                 lhsT_scale=q_scale[:, m * P : (m + 1) * P],
-                rhs=k_code[0][:, n0 : n0 + width].bitcast(FP8X4),
+                rhs=k_code[n0 // half][:, n0 % half : n0 % half + width].bitcast(FP8X4),
                 rhs_scale=k_scale[:, n0 : n0 + width],
                 start=True,
                 stop=True,
@@ -100,7 +96,7 @@ def tile_attend_lq_maxsim_kernel(tc, qT, k_words, k_scales, offq, offs, out):
             )
             if m == 0 and n0 + width == N:
                 nc.sync.dma_start(out[0, 0:P, :], best[0][:])
-            if m == 1 and n0 + 2 * width == N:
+            if m == 1 and n0 + width == 768:
                 nc.scalar.dma_start(out[0, P:NQ, 0:48], best[1][:, 0:48])
             if m == 1 and n0 + width == N:
                 nc.sync.dma_start(out[0, P:NQ, 48:64], best[1][:, 48:64])

@@ -76,7 +76,7 @@ def tile_attend_lq_maxsim_kernel(tc, qT, k_words, k_scales, offq, offs, out):
             nc.vector.tensor_copy(k_code[h][:], word_pool[:].indirect(k_list[:, h * half // 16 : (h + 1) * half // 16]))
 
         best = [keep.tile([P, N // SEG], F32, name="best%d" % m) for m in range(2)]
-        pieces = [(0, 0, 256), (0, 256, 256), (1, 0, 512), (0, 512, 512), (1, 512, 256), (1, 768, 256)]
+        pieces = [(m, h * half + n0, 256) for h in range(2) for m in range(2) for n0 in range(0, half, 256)]
         for i, (m, n0, width) in enumerate(pieces):
             acc = psum.tile([P, width], F32, name="acc%d" % i, tag="acc%d" % i)
             nc.tensor.matmul_mx(

@@ -76,9 +76,10 @@ def tile_attend_lq_maxsim_kernel(tc, qT, k_words, k_scales, offq, offs, out):
             nc.vector.tensor_copy(k_code[h][:], word_pool[:].indirect(k_list[:, h * half // 16 : (h + 1) * half // 16]))
 
         best = [keep.tile([P, N // SEG], F32, name="best%d" % m) for m in range(2)]
-        pieces = [(m, h * half + n0, 256) for h in range(2) for m in range(2) for n0 in range(0, half, 256)]
+        pieces = [(0, 0, 128), (0, 128, 128), (0, 256, 256), (1, 0, 256), (1, 256, 256), (0, 512, 256), (0, 768, 256)]
+        pieces = pieces + [(1, 512, 256), (1, 768, 128), (1, 896, 128)]
         for i, (m, n0, width) in enumerate(pieces):
-            acc = psum.tile([P, width], F32, name="acc%d" % i, tag="acc%d" % i)
+            acc = psum.tile([P, width], F32, name="acc%d" % i, tag="acc%d" % (i % 8))
             nc.tensor.matmul_mx(
                 out=acc[:],
                 lhsT=q_code[:, m * P : (m + 1) * P].bitcast(FP8X4),

@@ -53,7 +53,7 @@ def tile_attend_lq_maxsim_kernel(tc, qT, k_words, k_scales, offq, offs, out):
         picked_scale = keep.tile([P, N], U8, name="picked_scale", align_bytes=64)
         nc.vector.tensor_copy(picked_scale[:], scale_pool[:].indirect(k_list[:]))
         for r in range(4):
-            nc.scalar.dma_start(
+            (nc.scalar if r % 2 == 0 else nc.sync).dma_start(
                 k_scale[r:P:32, :].bitcast(I32),
                 picked_scale[11 + 7 * r : 11 + 7 * r + 28 * 3 + 1 : 28, :].bitcast(I32),
             )

@@ -17,6 +17,10 @@ POOL_K = 4096
 NQ = 256
 N = 1024
 SEG = 16
+HALF = N // 2
+ROW0 = 11
+ROW_STEP = 7
+WARM_M = 64
 
 FLOPS = 2 * NQ * N * P * PACK
 
@@ -30,65 +34,79 @@ def tile_attend_lq_maxsim_kernel(tc, qT, k_words, k_scales, offq, offs, out):
         q_list = keep.tile([P, NQ // 16], U16, name="q_list")
         k_list = keep.tile([P, N // 16], U16, name="k_list")
         q_rows = qT.rearrange("(p t) n -> p t n", t=PACK)
-        q_first = keep.tile([P, 2, POOL_Q], F32, name="q_first")
-        q_pool = keep.tile([P, 2, POOL_Q], F32, name="q_pool")
+        q_first = keep.tile([P, POOL_Q], F32, name="q_first")
+        q_rest = keep.tile([P, PACK - 1, POOL_Q], F32, name="q_rest")
         word_pool = keep.tile([P, POOL_K], U32, name="word_pool", align_bytes=64)
         scale_pool = keep.tile([P, POOL_K], U8, name="scale_pool", align_bytes=64)
 
-        nc.vector.memset(scale_pool[:].bitcast(I32), 0)
+        nc.vector.memset(scale_pool[:, 0 : POOL_K * 5 // 8].bitcast(I32), 0)
+        nc.gpsimd.memset(scale_pool[:, POOL_K * 5 // 8 : POOL_K].bitcast(I32), 0)
         words = k_words[0].rearrange("p n r -> p (n r)").bitcast(I32)
-        nc.scalar.dma_start(q_first[:], q_rows[:, 0:2, :])
-        nc.sync.dma_start(k_list[:], offs)
+        nc.scalar.dma_start(q_first[:], q_rows[:, 0, :])
         nc.sync.dma_start(q_list[:], offq)
-        nc.scalar.dma_start(scale_pool[11 : 11 + 7 * 15 + 1 : 7, :].bitcast(I32), k_scales[0].bitcast(I32))
-        nc.scalar.dma_start(q_pool[:], q_rows[:, 2:4, :])
+        nc.sync.dma_start(k_list[:], offs)
+        nc.scalar.dma_start(
+            scale_pool[ROW0 : ROW0 + ROW_STEP * 15 + 1 : ROW_STEP, :].bitcast(I32), k_scales[0].bitcast(I32)
+        )
+        nc.scalar.dma_start(q_rest[:], q_rows[:, 1:PACK, :])
         nc.scalar.dma_start(word_pool[:].bitcast(I32), words)
 
-        q_grouped = [keep.tile([P, P, PACK], BF16, name="q_grouped%d" % m, align_bytes=64) for m in range(2)]
-        for m in range(2):
-            for t in range(2):
-                nc.vector.tensor_copy(q_grouped[m][:, :, t], q_first[:, t, :].indirect(q_list[:, m * 8 : (m + 1) * 8]))
+        q_grouped = keep.tile([P, NQ, PACK], BF16, name="q_grouped", align_bytes=64)
+        nc.vector.tensor_copy(q_grouped[:, :, 0], q_first[:].indirect(q_list[:]))
 
         k_scale = keep.tile([P, N], U8, name="k_scale", align_bytes=64)
         picked_scale = keep.tile([P, N], U8, name="picked_scale", align_bytes=64)
         nc.vector.tensor_copy(picked_scale[:], scale_pool[:].indirect(k_list[:]))
         for r in range(4):
+            first = ROW0 + ROW_STEP * r
             (nc.scalar if r % 2 == 0 else nc.sync).dma_start(
                 k_scale[r:P:32, :].bitcast(I32),
-                picked_scale[11 + 7 * r : 11 + 7 * r + 28 * 3 + 1 : 28, :].bitcast(I32),
+                picked_scale[first : first + 4 * ROW_STEP * 3 + 1 : 4 * ROW_STEP, :].bitcast(I32),
             )
 
-        q_code = keep.tile([P, NQ], U32, name="q_code", align_bytes=64)
-        q_scale = keep.tile([P, NQ], U8, name="q_scale", align_bytes=64)
-        for m in range(2):
-            for t in range(2, PACK):
-                nc.vector.tensor_copy(q_grouped[m][:, :, t], q_pool[:, t - 2, :].indirect(q_list[:, m * 8 : (m + 1) * 8]))
-        for m in range(2):
+        for t in range(1, PACK):
+            nc.vector.tensor_copy(q_grouped[:, :, t], q_rest[:, t - 1, :].indirect(q_list[:]))
+        q_code = keep.tile([P, 2 * NQ], U32, name="q_code", align_bytes=64)
+        q_scale = keep.tile([P, 2 * NQ], U8, name="q_scale", align_bytes=64)
+        for c in (0, NQ):
             nc.vector.quantize_mx(
-                out=q_code[:, m * P : (m + 1) * P].bitcast(FP8X4),
-                scales=q_scale[:, m * P : (m + 1) * P],
-                in_=q_grouped[m][:].rearrange("p n t -> p (n t)"),
+                out=q_code[:, c : c + NQ].bitcast(FP8X4),
+                scales=q_scale[:, c : c + NQ],
+                in_=q_grouped[:].rearrange("p n t -> p (n t)"),
             )
 
-        half = N // 2
-        k_code = [keep.tile([P, half], U32, name="k_code%d" % h, align_bytes=64) for h in range(2)]
-        for h in range(2):
-            nc.vector.tensor_copy(k_code[h][:], word_pool[:].indirect(k_list[:, h * half // 16 : (h + 1) * half // 16]))
-
-        best = [keep.tile([P, N // SEG], F32, name="best%d" % m) for m in range(2)]
-        pieces = [(0, 0, 128), (0, 128, 128), (0, 256, 256), (1, 0, 256), (1, 256, 256), (0, 512, 256), (0, 768, 256)]
-        pieces = pieces + [(1, 512, 256), (1, 768, 128), (1, 896, 128)]
-        for i, (m, n0, width) in enumerate(pieces):
-            acc = psum.tile([P, width], F32, name="acc%d" % i, tag="acc%d" % (i % 8))
+        warm = psum.tile([WARM_M, HALF], F32, name="warm")
+        for w in range(2):
             nc.tensor.matmul_mx(
-                out=acc[:],
-                lhsT=q_code[:, m * P : (m + 1) * P].bitcast(FP8X4),
-                lhsT_scale=q_scale[:, m * P : (m + 1) * P],
-                rhs=k_code[n0 // half][:, n0 % half : n0 % half + width].bitcast(FP8X4),
-                rhs_scale=k_scale[:, n0 : n0 + width],
+                out=warm[:],
+                lhsT=q_code[:, w * WARM_M : (w + 1) * WARM_M].bitcast(FP8X4),
+                lhsT_scale=q_scale[:, w * WARM_M : (w + 1) * WARM_M],
+                rhs=q_code[:].bitcast(FP8X4),
+                rhs_scale=q_scale[:],
                 start=True,
                 stop=True,
             )
+
+        k_code = [keep.tile([P, HALF], U32, name="k_code%d" % h, align_bytes=64) for h in range(2)]
+        for h in range(2):
+            nc.vector.tensor_copy(k_code[h][:], word_pool[:].indirect(k_list[:, h * HALF // 16 : (h + 1) * HALF // 16]))
+
+        best = [keep.tile([P, N // SEG], F32, name="best%d" % m) for m in range(2)]
+        banks = [(0, 0, 256, 128), (0, 256, 256, 128), (1, 0, 256, 128), (1, 256, 256, 128)]
+        banks = banks + [(0, 512, 512, 128), (1, 512, 384, 64), (1, 896, 128, 64)]
+        for i, (m, n0, width, step) in enumerate(banks):
+            acc = psum.tile([P, width], F32, name="acc%d" % i)
+            for c in range(0, width, step):
+                n1 = n0 + c
+                nc.tensor.matmul_mx(
+                    out=acc[:, c : c + step],
+                    lhsT=q_code[:, m * P : (m + 1) * P].bitcast(FP8X4),
+                    lhsT_scale=q_scale[:, m * P : (m + 1) * P],
+                    rhs=k_code[n1 // HALF][:, n1 % HALF : n1 % HALF + step].bitcast(FP8X4),
+                    rhs_scale=k_scale[:, n1 : n1 + step],
+                    start=True,
+                    stop=True,
+                )
             nc.vector.tensor_reduce(
                 out=best[m][:, n0 // SEG : (n0 + width) // SEG],
                 in_=acc[:].rearrange("p (j s) -> p j s", s=SEG),
@@ -97,7 +115,7 @@ def tile_attend_lq_maxsim_kernel(tc, qT, k_words, k_scales, offq, offs, out):
             )
             if m == 0 and n0 + width == N:
                 nc.sync.dma_start(out[0, 0:P, :], best[0][:])
-            if m == 1 and n0 + width == 768:
-                nc.scalar.dma_start(out[0, P:NQ, 0:48], best[1][:, 0:48])
+            if m == 1 and n0 + width == 896:
+                nc.scalar.dma_start(out[0, P:NQ, 0:56], best[1][:, 0:56])
             if m == 1 and n0 + width == N:
-                nc.sync.dma_start(out[0, P:NQ, 48:64], best[1][:, 48:64])
+                nc.sync.dma_start(out[0, P:NQ, 56:64], best[1][:, 56:64])

@@ -59,7 +59,7 @@ def tile_attend_lq_maxsim_kernel(tc, qT, k_words, k_scales, offq, offs, out):
         nc.vector.tensor_copy(picked_scale[:], scale_pool[:].indirect(k_list[:]))
         for r in range(4):
             first = ROW0 + ROW_STEP * r
-            (nc.scalar if r % 2 == 0 else nc.sync).dma_start(
+            nc.scalar.dma_start(
                 k_scale[r:P:32, :].bitcast(I32),
                 picked_scale[first : first + 4 * ROW_STEP * 3 + 1 : 4 * ROW_STEP, :].bitcast(I32),
             )

@@ -17,10 +17,10 @@ POOL_K = 4096
 NQ = 256
 N = 1024
 SEG = 16
-HALF = N // 2
 ROW0 = 11
 ROW_STEP = 7
-WARM_M = 64
+GATHERS = (256, 256, 512)
+WIDTHS = (128, 256, 256)
 
 FLOPS = 2 * NQ * N * P * PACK
 
@@ -29,30 +29,29 @@ def tile_attend_lq_maxsim_kernel(tc, qT, k_words, k_scales, offq, offs, out):
     nc = tc.nc
     with ExitStack() as ctx:
         keep = ctx.enter_context(tc.tile_pool(name="keep", bufs=1))
-        psum = ctx.enter_context(tc.psum_pool(name="psum", bufs=1))
+        psum = ctx.enter_context(tc.psum_pool(name="psum", bufs=8))
 
         q_list = keep.tile([P, NQ // 16], U16, name="q_list")
         k_list = keep.tile([P, N // 16], U16, name="k_list")
         q_rows = qT.rearrange("(p t) n -> p t n", t=PACK)
-        q_first = keep.tile([P, POOL_Q], F32, name="q_first")
-        q_rest = keep.tile([P, PACK - 1, POOL_Q], F32, name="q_rest")
+        q_pool = [keep.tile([P, 2, POOL_Q], F32, name="q_pool%d" % u) for u in range(2)]
         word_pool = keep.tile([P, POOL_K], U32, name="word_pool", align_bytes=64)
         scale_pool = keep.tile([P, POOL_K], U8, name="scale_pool", align_bytes=64)
 
-        nc.vector.memset(scale_pool[:, 0 : POOL_K * 5 // 8].bitcast(I32), 0)
-        nc.gpsimd.memset(scale_pool[:, POOL_K * 5 // 8 : POOL_K].bitcast(I32), 0)
+        nc.vector.memset(scale_pool[:].bitcast(I32), 0)
         words = k_words[0].rearrange("p n r -> p (n r)").bitcast(I32)
-        nc.scalar.dma_start(q_first[:], q_rows[:, 0, :])
+        nc.scalar.dma_start(q_pool[0][:], q_rows[:, 0:2, :])
         nc.sync.dma_start(q_list[:], offq)
         nc.sync.dma_start(k_list[:], offs)
         nc.scalar.dma_start(
             scale_pool[ROW0 : ROW0 + ROW_STEP * 15 + 1 : ROW_STEP, :].bitcast(I32), k_scales[0].bitcast(I32)
         )
-        nc.scalar.dma_start(q_rest[:], q_rows[:, 1:PACK, :])
+        nc.scalar.dma_start(q_pool[1][:], q_rows[:, 2:4, :])
         nc.scalar.dma_start(word_pool[:].bitcast(I32), words)
 
         q_grouped = keep.tile([P, NQ, PACK], BF16, name="q_grouped", align_bytes=64)
-        nc.vector.tensor_copy(q_grouped[:, :, 0], q_first[:].indirect(q_list[:]))
+        for t in range(2):
+            nc.vector.tensor_copy(q_grouped[:, :, t], q_pool[0][:, t, :].indirect(q_list[:]))
 
         k_scale = keep.tile([P, N], U8, name="k_scale", align_bytes=64)
         picked_scale = keep.tile([P, N], U8, name="picked_scale", align_bytes=64)
@@ -64,58 +63,52 @@ def tile_attend_lq_maxsim_kernel(tc, qT, k_words, k_scales, offq, offs, out):
                 picked_scale[first : first + 4 * ROW_STEP * 3 + 1 : 4 * ROW_STEP, :].bitcast(I32),
             )
 
-        for t in range(1, PACK):
-            nc.vector.tensor_copy(q_grouped[:, :, t], q_rest[:, t - 1, :].indirect(q_list[:]))
-        q_code = keep.tile([P, 2 * NQ], U32, name="q_code", align_bytes=64)
-        q_scale = keep.tile([P, 2 * NQ], U8, name="q_scale", align_bytes=64)
-        for c in (0, NQ):
-            nc.vector.quantize_mx(
-                out=q_code[:, c : c + NQ].bitcast(FP8X4),
-                scales=q_scale[:, c : c + NQ],
-                in_=q_grouped[:].rearrange("p n t -> p (n t)"),
-            )
+        for t in range(2):
+            nc.vector.tensor_copy(q_grouped[:, :, 2 + t], q_pool[1][:, t, :].indirect(q_list[:]))
+        q_code = keep.tile([P, NQ], U32, name="q_code", align_bytes=64)
+        q_scale = keep.tile([P, NQ], U8, name="q_scale", align_bytes=64)
+        nc.vector.quantize_mx(
+            out=q_code[:].bitcast(FP8X4),
+            scales=q_scale[:],
+            in_=q_grouped[:].rearrange("p n t -> p (n t)"),
+        )
 
-        warm = psum.tile([WARM_M, HALF], F32, name="warm")
-        for w in range(2):
-            nc.tensor.matmul_mx(
-                out=warm[:],
-                lhsT=q_code[:, w * WARM_M : (w + 1) * WARM_M].bitcast(FP8X4),
-                lhsT_scale=q_scale[:, w * WARM_M : (w + 1) * WARM_M],
-                rhs=q_code[:].bitcast(FP8X4),
-                rhs_scale=q_scale[:],
-                start=True,
-                stop=True,
-            )
-
-        k_code = [keep.tile([P, HALF], U32, name="k_code%d" % h, align_bytes=64) for h in range(2)]
-        for h in range(2):
-            nc.vector.tensor_copy(k_code[h][:], word_pool[:].indirect(k_list[:, h * HALF // 16 : (h + 1) * HALF // 16]))
+        k_code = []
+        first = 0
+        for g, count in enumerate(GATHERS):
+            codes = keep.tile([P, count], U32, name="k_code%d" % g, align_bytes=64)
+            nc.vector.tensor_copy(codes[:], word_pool[:].indirect(k_list[:, first // 16 : (first + count) // 16]))
+            k_code.append(codes)
+            first = first + count
 
         best = [keep.tile([P, N // SEG], F32, name="best%d" % m) for m in range(2)]
-        banks = [(0, 0, 256, 128), (0, 256, 256, 128), (1, 0, 256, 128), (1, 256, 256, 128)]
-        banks = banks + [(0, 512, 512, 128), (1, 512, 384, 64), (1, 896, 128, 64)]
-        for i, (m, n0, width, step) in enumerate(banks):
-            acc = psum.tile([P, width], F32, name="acc%d" % i)
-            for c in range(0, width, step):
-                n1 = n0 + c
-                nc.tensor.matmul_mx(
-                    out=acc[:, c : c + step],
-                    lhsT=q_code[:, m * P : (m + 1) * P].bitcast(FP8X4),
-                    lhsT_scale=q_scale[:, m * P : (m + 1) * P],
-                    rhs=k_code[n1 // HALF][:, n1 % HALF : n1 % HALF + step].bitcast(FP8X4),
-                    rhs_scale=k_scale[:, n1 : n1 + step],
-                    start=True,
-                    stop=True,
-                )
-            nc.vector.tensor_reduce(
-                out=best[m][:, n0 // SEG : (n0 + width) // SEG],
-                in_=acc[:].rearrange("p (j s) -> p j s", s=SEG),
-                axis=mybir.AxisListType.X,
-                op=mybir.AluOpType.max,
-            )
-            if m == 0 and n0 + width == N:
-                nc.sync.dma_start(out[0, 0:P, :], best[0][:])
-            if m == 1 and n0 + width == 896:
-                nc.scalar.dma_start(out[0, P:NQ, 0:56], best[1][:, 0:56])
-            if m == 1 and n0 + width == N:
-                nc.sync.dma_start(out[0, P:NQ, 56:64], best[1][:, 56:64])
+        first = 0
+        for g, count in enumerate(GATHERS):
+            width = WIDTHS[g]
+            for m in range(2):
+                for c in range(0, count, width):
+                    n0 = first + c
+                    acc = psum.tile([P, width], F32, name="acc")
+                    nc.tensor.matmul_mx(
+                        out=acc[:],
+                        lhsT=q_code[:, m * P : (m + 1) * P].bitcast(FP8X4),
+                        lhsT_scale=q_scale[:, m * P : (m + 1) * P],
+                        rhs=k_code[g][:, c : c + width].bitcast(FP8X4),
+                        rhs_scale=k_scale[:, n0 : n0 + width],
+                        start=True,
+                        stop=True,
+                    )
+                    nc.vector.tensor_reduce(
+                        out=best[m][:, n0 // SEG : (n0 + width) // SEG],
+                        in_=acc[:].rearrange("p (j s) -> p j s", s=SEG),
+                        axis=mybir.AxisListType.X,
+                        op=mybir.AluOpType.max,
+                    )
+                    done = (n0 + width) // SEG
+                    if m == 0 and done == 64:
+                        nc.sync.dma_start(out[0, 0:P, :], best[0][:])
+                    if m == 1 and done == 48:
+                        nc.scalar.dma_start(out[0, P:NQ, 0:48], best[1][:, 0:48])
+                    if m == 1 and done == 64:
+                        nc.sync.dma_start(out[0, P:NQ, 48:64], best[1][:, 48:64])
+            first = first + count

@@ -19,6 +19,7 @@ N = 1024
 SEG = 16
 ROW0 = 11
 ROW_STEP = 7
+ZERO_SPLIT = POOL_K * 5 // 8
 GATHERS = (256, 256, 512)
 WIDTHS = (128, 256, 256)
 
@@ -34,24 +35,25 @@ def tile_attend_lq_maxsim_kernel(tc, qT, k_words, k_scales, offq, offs, out):
         q_list = keep.tile([P, NQ // 16], U16, name="q_list")
         k_list = keep.tile([P, N // 16], U16, name="k_list")
         q_rows = qT.rearrange("(p t) n -> p t n", t=PACK)
-        q_pool = [keep.tile([P, 2, POOL_Q], F32, name="q_pool%d" % u) for u in range(2)]
+        q_first = keep.tile([P, POOL_Q], F32, name="q_first")
+        q_rest = keep.tile([P, PACK - 1, POOL_Q], F32, name="q_rest")
         word_pool = keep.tile([P, POOL_K], U32, name="word_pool", align_bytes=64)
         scale_pool = keep.tile([P, POOL_K], U8, name="scale_pool", align_bytes=64)
 
-        nc.vector.memset(scale_pool[:].bitcast(I32), 0)
+        nc.vector.memset(scale_pool[:, 0:ZERO_SPLIT].bitcast(I32), 0)
+        nc.gpsimd.memset(scale_pool[:, ZERO_SPLIT:POOL_K].bitcast(I32), 0)
         words = k_words[0].rearrange("p n r -> p (n r)").bitcast(I32)
-        nc.scalar.dma_start(q_pool[0][:], q_rows[:, 0:2, :])
+        nc.scalar.dma_start(q_first[:], q_rows[:, 0, :])
         nc.sync.dma_start(q_list[:], offq)
         nc.sync.dma_start(k_list[:], offs)
         nc.scalar.dma_start(
             scale_pool[ROW0 : ROW0 + ROW_STEP * 15 + 1 : ROW_STEP, :].bitcast(I32), k_scales[0].bitcast(I32)
         )
-        nc.scalar.dma_start(q_pool[1][:], q_rows[:, 2:4, :])
+        nc.scalar.dma_start(q_rest[:], q_rows[:, 1:PACK, :])
         nc.scalar.dma_start(word_pool[:].bitcast(I32), words)
 
         q_grouped = keep.tile([P, NQ, PACK], BF16, name="q_grouped", align_bytes=64)
-        for t in range(2):
-            nc.vector.tensor_copy(q_grouped[:, :, t], q_pool[0][:, t, :].indirect(q_list[:]))
+        nc.vector.tensor_copy(q_grouped[:, :, 0], q_first[:].indirect(q_list[:]))
 
         k_scale = keep.tile([P, N], U8, name="k_scale", align_bytes=64)
         picked_scale = keep.tile([P, N], U8, name="picked_scale", align_bytes=64)
@@ -63,8 +65,8 @@ def tile_attend_lq_maxsim_kernel(tc, qT, k_words, k_scales, offq, offs, out):
                 picked_scale[first : first + 4 * ROW_STEP * 3 + 1 : 4 * ROW_STEP, :].bitcast(I32),
             )
 
-        for t in range(2):
-            nc.vector.tensor_copy(q_grouped[:, :, 2 + t], q_pool[1][:, t, :].indirect(q_list[:]))
+        for t in range(1, PACK):
+            nc.vector.tensor_copy(q_grouped[:, :, t], q_rest[:, t - 1, :].indirect(q_list[:]))
         q_code = keep.tile([P, NQ], U32, name="q_code", align_bytes=64)
         q_scale = keep.tile([P, NQ], U8, name="q_scale", align_bytes=64)
         nc.vector.quantize_mx(

@@ -35,10 +35,10 @@ def tile_attend_lq_maxsim_kernel(tc, qT, k_words, k_scales, offq, offs, out):
         q_list = keep.tile([P, NQ // 16], U16, name="q_list")
         k_list = keep.tile([P, N // 16], U16, name="k_list")
         q_rows = qT.rearrange("(p t) n -> p t n", t=PACK)
-        q_first = keep.tile([P, POOL_Q], F32, name="q_first")
-        q_rest = keep.tile([P, PACK - 1, POOL_Q], F32, name="q_rest")
-        word_pool = keep.tile([P, POOL_K], U32, name="word_pool", align_bytes=64)
-        scale_pool = keep.tile([P, POOL_K], U8, name="scale_pool", align_bytes=64)
+        q_first = keep.tile([P, POOL_Q], F32, name="q_first", align_bytes=256)
+        q_rest = keep.tile([P, PACK - 1, POOL_Q], F32, name="q_rest", align_bytes=256)
+        word_pool = keep.tile([P, POOL_K], U32, name="word_pool", align_bytes=256)
+        scale_pool = keep.tile([P, POOL_K], U8, name="scale_pool", align_bytes=256)
 
         nc.vector.memset(scale_pool[:, 0:ZERO_SPLIT].bitcast(I32), 0)
         nc.gpsimd.memset(scale_pool[:, ZERO_SPLIT:POOL_K].bitcast(I32), 0)

from contextlib import ExitStack

import concourse.mybir as mybir

F32 = mybir.dt.float32
BF16 = mybir.dt.bfloat16
I32 = mybir.dt.int32
U32 = mybir.dt.uint32
U16 = mybir.dt.uint16
U8 = mybir.dt.uint8
FP8X4 = mybir.dt.float8_e4m3fn_x4

P = 128
PACK = 4
POOL_Q = 1024
POOL_K = 4096
NQ = 256
N = 1024
SEG = 16
ROW0 = 11
ROW_STEP = 7
ZERO_SPLIT = POOL_K * 5 // 8
GATHERS = (256, 256, 512)
WIDTHS = (128, 256, 256)

FLOPS = 2 * NQ * N * P * PACK


def tile_attend_lq_maxsim_kernel(tc, qT, k_words, k_scales, offq, offs, out):
    nc = tc.nc
    with ExitStack() as ctx:
        keep = ctx.enter_context(tc.tile_pool(name="keep", bufs=1))
        psum = ctx.enter_context(tc.psum_pool(name="psum", bufs=8))

        q_list = keep.tile([P, NQ // 16], U16, name="q_list")
        k_list = keep.tile([P, N // 16], U16, name="k_list")
        q_rows = qT.rearrange("(p t) n -> p t n", t=PACK)
        q_first = keep.tile([P, POOL_Q], F32, name="q_first", align_bytes=256)
        q_rest = keep.tile([P, PACK - 1, POOL_Q], F32, name="q_rest", align_bytes=256)
        word_pool = keep.tile([P, POOL_K], U32, name="word_pool", align_bytes=256)
        scale_pool = keep.tile([P, POOL_K], U8, name="scale_pool", align_bytes=256)

        nc.vector.memset(scale_pool[:, 0:ZERO_SPLIT].bitcast(I32), 0)
        nc.gpsimd.memset(scale_pool[:, ZERO_SPLIT:POOL_K].bitcast(I32), 0)
        words = k_words[0].rearrange("p n r -> p (n r)").bitcast(I32)
        nc.scalar.dma_start(q_first[:], q_rows[:, 0, :])
        nc.sync.dma_start(q_list[:], offq)
        nc.sync.dma_start(k_list[:], offs)
        nc.scalar.dma_start(
            scale_pool[ROW0 : ROW0 + ROW_STEP * 15 + 1 : ROW_STEP, :].bitcast(I32), k_scales[0].bitcast(I32)
        )
        nc.scalar.dma_start(q_rest[:], q_rows[:, 1:PACK, :])
        nc.scalar.dma_start(word_pool[:].bitcast(I32), words)

        q_grouped = keep.tile([P, NQ, PACK], BF16, name="q_grouped", align_bytes=64)
        nc.vector.tensor_copy(q_grouped[:, :, 0], q_first[:].indirect(q_list[:]))

        k_scale = keep.tile([P, N], U8, name="k_scale", align_bytes=64)
        picked_scale = keep.tile([P, N], U8, name="picked_scale", align_bytes=64)
        nc.vector.tensor_copy(picked_scale[:], scale_pool[:].indirect(k_list[:]))
        for r in range(4):
            first = ROW0 + ROW_STEP * r
            nc.scalar.dma_start(
                k_scale[r:P:32, :].bitcast(I32),
                picked_scale[first : first + 4 * ROW_STEP * 3 + 1 : 4 * ROW_STEP, :].bitcast(I32),
            )

        for t in range(1, PACK):
            nc.vector.tensor_copy(q_grouped[:, :, t], q_rest[:, t - 1, :].indirect(q_list[:]))
        q_code = keep.tile([P, NQ], U32, name="q_code", align_bytes=64)
        q_scale = keep.tile([P, NQ], U8, name="q_scale", align_bytes=64)
        nc.vector.quantize_mx(
            out=q_code[:].bitcast(FP8X4),
            scales=q_scale[:],
            in_=q_grouped[:].rearrange("p n t -> p (n t)"),
        )

        k_code = []
        first = 0
        for g, count in enumerate(GATHERS):
            codes = keep.tile([P, count], U32, name="k_code%d" % g, align_bytes=64)
            nc.vector.tensor_copy(codes[:], word_pool[:].indirect(k_list[:, first // 16 : (first + count) // 16]))
            k_code.append(codes)
            first = first + count

        best = [keep.tile([P, N // SEG], F32, name="best%d" % m) for m in range(2)]
        first = 0
        for g, count in enumerate(GATHERS):
            width = WIDTHS[g]
            for m in range(2):
                for c in range(0, count, width):
                    n0 = first + c
                    acc = psum.tile([P, width], F32, name="acc")
                    nc.tensor.matmul_mx(
                        out=acc[:],
                        lhsT=q_code[:, m * P : (m + 1) * P].bitcast(FP8X4),
                        lhsT_scale=q_scale[:, m * P : (m + 1) * P],
                        rhs=k_code[g][:, c : c + width].bitcast(FP8X4),
                        rhs_scale=k_scale[:, n0 : n0 + width],
                        start=True,
                        stop=True,
                    )
                    nc.vector.tensor_reduce(
                        out=best[m][:, n0 // SEG : (n0 + width) // SEG],
                        in_=acc[:].rearrange("p (j s) -> p j s", s=SEG),
                        axis=mybir.AxisListType.X,
                        op=mybir.AluOpType.max,
                    )
                    done = (n0 + width) // SEG
                    if m == 0 and done == 64:
                        nc.sync.dma_start(out[0, 0:P, :], best[0][:])
                    if m == 1 and done == 48:
                        nc.scalar.dma_start(out[0, P:NQ, 0:48], best[1][:, 0:48])
                    if m == 1 and done == 64:
                        nc.sync.dma_start(out[0, P:NQ, 48:64], best[1][:, 48:64])
            first = first + count
